import numpy as np, ml_dtypes
CORES = [50,52,122,124]
N = 4
import mx_ref
NC = 128
BF = ml_dtypes.bfloat16
def cut(t, i, w=512):
    return t[:, w * i:w * i + w]
def term(a, B):
    return np.stack([mx_ref.matmul(mx_ref.quantize(cut(a, i)), B) for i in range(4)], axis=2).reshape(128, -1)
def setup_inputs(rng):
    def f(*shape):
        return mx_ref.flush((rng.standard_normal(shape, dtype=np.float32) * np.exp2(rng.integers(-2, 3, shape[:-1] + (1,)))).astype(BF))
    return {"a": f(N, 128, 4 * 512), "b": f(N, 128, 2 * 4 * NC)}
def setup_inputs_blocks(rng):
    d = setup_inputs(rng)
    for k in ("a", "b"): d[k] = mx_ref.spread(d[k], rng, 2)
    return d
def setup_inputs_wide(rng):
    d = setup_inputs(rng)
    for k in ("a", "b"): d[k] = mx_ref.flush((d[k].astype(np.float32) * np.exp2(rng.integers(-4, 5, (N, 1, 1))).astype(np.float32)).astype(BF))
    return d
def setup_inputs_lossless(rng):
    a = np.zeros((N, 128, 4 * 128, 4), np.float32)
    for r in range(N):
        k = rng.integers(0, 512, size=4 * 128)
        a[r, k // 4, np.arange(4 * 128), k % 4] = 1.0
    size = np.tile(np.repeat(2.0 ** rng.integers(-4, 5, size=(1, 1, NC)), 4, axis=2), (1, 1, 2))
    b = rng.integers(-1, 2, size=(N, 128, 2 * 4 * NC)) * size
    return {"a": a.reshape(N, 128, 4 * 512).astype(BF), "b": b.astype(np.float32).astype(BF)}
def reference(a, b):
    T = [term(a[r], mx_ref.quantize(cut(b[r], k, 4 * NC))) for r in range(N) for k in range(2)]
    y = np.zeros((N, 128, 4 * NC), np.float32)
    for c in range(N):
        y[c] = mx_ref.total(T[:2 * c + 2])
    return {"y": y}

@@ -1,0 +1,201 @@
+from concourse.bass import DstId, RemoteDMATransfer
+from concourse.mybir import dt, AluOpType, ActivationFunctionType
+
+W = 512
+NW = 128
+BANK = 512
+
+SCRATCH = {
+    "ta": ("sbuf", [128, 4 * W], "bfloat16"),
+    "tb": ("sbuf", [128, 2 * W], "bfloat16"),
+    "z": ("sbuf", [128, W + 4], "bfloat16"),
+    "h": ("sbuf", [128, W], "bfloat16"),
+    "hs": ("sbuf", [128, W], "bfloat16"),
+    "yt": ("sbuf", [128, W], "float32"),
+    "ps": ("psum", [128, 8 * BANK], "float32"),
+}
+for _n, _w in (("a", 4 * NW), ("b", 2 * NW), ("e", 4 * NW), ("h", NW), ("s", NW), ("l0", NW), ("l1", NW)):
+    SCRATCH["q" + _n] = ("sbuf", [128, _w], "float8_e4m3fn_x4")
+    SCRATCH["s" + _n] = ("sbuf", [128, _w], "uint8")
+
+SEMAPHORES = (["ld_b", "ld_a", "ld_a3", "z_one", "z_sel", "q_b", "q_e", "q_h", "q_s", "stored", "left"]
+              + ["%s%d" % (n, i) for n in ("q_a", "mm", "ch", "cy", "cs", "fin") for i in range(4)]
+              + ["l0_q", "l0_s", "l1_q", "l1_s"])
+
+
+def _count(mask):
+    return bin(mask).count("1")
+
+
+def _helper(T, topo):
+    c1, c2 = T.cores[1], T.cores[2]
+    for c in range(128):
+        if (topo.chip(c) == topo.chip(c1) and topo.die(c) == topo.die(c1) and T.rank_of(c) is None
+                and topo.may_write(c, c2)):
+            return c
+    return None
+
+
+def rank_program(g, core, T, topo):
+    rank = T.rank_of(core)
+    helper = _helper(T, topo)
+    if rank is None and core != helper:
+        return
+    R = T.cores
+    S = T.sem
+    left = [0]
+
+    def codes(n):
+        return T["q" + n][:].bitcast(dt.uint8)
+
+    def scales(n):
+        return T["s" + n][:]
+
+    def send(dst, what, land, src, mask):
+        view = codes if what == "q" else scales
+        rid, pid, _ = topo.addr(dst)
+        g.remote_dma(out_ap=view(land), in_ap=view(src), remote_sem=S["%s_%s" % (land, what)], local_sem=S["left"],
+                     pid=pid, routing_id=rid, dma_engine_mask=mask)
+        left[0] += _count(mask)
+
+    def send_two(pairs, what, land, src):
+        view = codes if what == "q" else scales
+        tr = []
+        for dst, mask in pairs:
+            rid, pid, _ = topo.addr(dst)
+            tr.append(RemoteDMATransfer(src=view(src), dst=view(land), dst_ids=[DstId(rid=rid, pnc=pid)],
+                                        dma_engine_mask=mask, remote_sem=S["%s_%s" % (land, what)]))
+            left[0] += _count(mask)
+        g.remote_dma_fused(tr, local_sem=S["left"])
+
+    m_far0 = topo.mask(R[0], R[2])
+    m_near0 = topo.mask(R[0], R[1]) & ~m_far0
+    m_10 = topo.mask(R[1], R[0])
+    m_1h = topo.mask(R[1], helper)
+    m_h2 = topo.mask(helper, R[2])
+    m_03 = topo.mask(R[0], R[3])
+    m_23 = topo.mask(R[2], R[3])
+    arrive = {0: {"l1": m_10}, 1: {"l0": m_near0}, 2: {"l0": m_far0, "l1": m_h2}, 3: {"l0": m_23, "l1": m_03}}
+
+    if rank is None:
+        for what in ("q", "s"):
+            g.wait_ge(S["l1_" + what], _count(m_1h))
+            send(R[2], what, "l1", "l1", m_h2)
+        g.wait_ge(S.left, left[0])
+        return
+
+    v, t, a, sy = g.vector, g.tensor, g.scalar, g.sync
+    COPY = ActivationFunctionType.Copy
+
+    def bank(i):
+        return T.ps[:, BANK * i:BANK * i + NW]
+
+    def col(buf, i):
+        return T[buf][:, i:W:4]
+
+    def piece(n, i):
+        return T["q" + n][:, NW * i:NW * i + NW], T["s" + n][:, NW * i:NW * i + NW]
+
+    def product(i, dest, stop):
+        qa, sa = piece("a", i)
+        for k in range(2):
+            qb, sb = piece("b", k)
+            m = t.matmul_mx(bank(dest), qa, sa, qb, sb, k == 0, stop and k == 1)
+        return m
+
+    sy.dma_start(T.tb[:], T.b[:]).then_inc(S.ld_b, 16)
+    a.dma_start(T.ta[:, 0:3 * W], T.a[:, 0:3 * W]).then_inc(S.ld_a, 16)
+    sy.dma_start(T.ta[:, 3 * W:4 * W], T.a[:, 3 * W:4 * W]).then_inc(S.ld_a3, 16)
+
+    v.memset(T.z[:], 1.0).then_inc(S.z_one, 1)
+    g.wait_ge(S.z_one, 1)
+    g.affine_select(T.z[:], T.z[:], [[-1, W + 4]], AluOpType.is_equal, 0.0, 3, 4).then_inc(S.z_sel, 1)
+
+    v.wait_ge(S.ld_b, 16)
+    v.quantize_mx(T.qb[:], T.sb[:], T.tb[:]).then_inc(S.q_b, 1)
+    t.wait_ge(S.q_b, 1)
+    for i in range(4):
+        if i == 0:
+            v.wait_ge(S.ld_a, 16)
+        if i == 3:
+            v.wait_ge(S.ld_a3, 16)
+        qa, sa = piece("a", i)
+        v.quantize_mx(qa, sa, T.ta[:, W * i:W * i + W]).then_inc(S["q_a%d" % i], 1)
+        t.wait_ge(S["q_a%d" % i], 1)
+        if rank < 3:
+            product(i, i, True).then_inc(S["mm%d" % i], 1)
+        else:
+            product(i, 4 + i, False)
+    if rank < 3:
+        for i in range(4):
+            product(i, 4 + i, False)
+
+    if rank < 3:
+        for i in range(3):
+            a.wait_ge(S["mm%d" % i], 1)
+            a.activation(col("h", i), bank(i), COPY).then_inc(S["ch%d" % i], 1)
+        v.wait_ge(S.mm3, 1)
+        v.tensor_copy(col("h", 3), bank(3)).then_inc(S.ch3, 1)
+        for i in range(4):
+            v.wait_ge(S["ch%d" % i], 1)
+        v.quantize_mx(T.qh[:], T.sh[:], T.h[:]).then_inc(S.q_h, 1)
+        g.wait_ge(S.q_h, 1)
+        if rank == 0:
+            for what in ("q", "s"):
+                send_two([(R[2], m_far0), (R[1], m_near0)], what, "l0", "h")
+        if rank == 1:
+            for what in ("q", "s"):
+                send(R[0], what, "l1", "h", m_10)
+            for what in ("q", "s"):
+                send(helper, what, "l1", "h", m_1h)
+        if rank == 2:
+            for what in ("q", "s"):
+                send(R[3], what, "l0", "h", m_23)
+
+    v.wait_ge(S.z_sel, 1)
+    for i in range(4):
+        qe, se = piece("e", i)
+        v.quantize_mx(qe, se, T.z[:, 3 - i:3 - i + W]).then_inc(S.q_e, 1)
+
+    if rank == 0:
+        a.wait_ge(S.ch3, 1)
+        for i in range(4):
+            a.wait_ge(S["mm%d" % i], 1)
+            a.activation(col("yt", i), bank(i), COPY).then_inc(S["cy%d" % i], 1)
+            sy.wait_ge(S["cy%d" % i], 1)
+        sy.dma_start(T.y[:], T.yt[:]).then_inc(S.stored, 16)
+
+    t.wait_ge(S.q_e, 4)
+    lands = sorted(arrive[rank])
+    for land in lands:
+        for what in ("q", "s"):
+            t.wait_ge(S["%s_%s" % (land, what)], _count(arrive[rank][land]))
+        ql, sl = T["q" + land][:], T["s" + land][:]
+        for i in range(4):
+            qe, se = piece("e", i)
+            last = land == lands[-1]
+            m = t.matmul_mx(bank(4 + i), qe, se, ql, sl, False, last)
+            if last:
+                m.then_inc(S["fin%d" % i], 1)
+
+    buf, cs = ("hs", "cs%d") if rank == 0 else ("yt", "cy%d")
+    for i in (0, 2):
+        a.wait_ge(S["fin%d" % i], 1)
+        a.activation(col(buf, i), bank(4 + i), COPY).then_inc(S[cs % i], 1)
+    for i in (1, 3):
+        v.wait_ge(S["fin%d" % i], 1)
+        v.tensor_copy(col(buf, i), bank(4 + i)).then_inc(S[cs % i], 1)
+    if rank == 0:
+        for i in range(4):
+            v.wait_ge(S[cs % i], 1)
+        v.quantize_mx(T.qs[:], T.ss[:], T.hs[:]).then_inc(S.q_s, 1)
+        g.wait_ge(S.q_s, 1)
+        for what in ("q", "s"):
+            send(R[3], what, "l1", "s", m_03)
+    else:
+        for i in range(4):
+            sy.wait_ge(S[cs % i], 1)
+        sy.dma_start(T.y[:], T.yt[:]).then_inc(S.stored, 16)
+    sy.wait_ge(S.stored, 16)
+    if left[0]:
+        g.wait_ge(S.left, left[0])

@@ -18,9 +18,11 @@ for _n, _w in (("a", 4 * NW), ("b", 2 * NW), ("e", 4 * NW), ("h", NW), ("s", NW)
     SCRATCH["q" + _n] = ("sbuf", [128, _w], "float8_e4m3fn_x4")
     SCRATCH["s" + _n] = ("sbuf", [128, _w], "uint8")
 
-SEMAPHORES = (["ld_b", "ld_a", "ld_a3", "z_one", "z_sel", "q_b", "q_e", "q_h", "q_s", "stored", "left"]
+SEMAPHORES = (["ld_b", "ld_a", "ld_a3", "z_one", "z_sel", "q_b", "q_e", "q_e0", "q_h", "q_s", "stored", "left"]
               + ["%s%d" % (n, i) for n in ("q_a", "mm", "ch", "cy", "cs", "fin") for i in range(4)]
-              + ["l0_q", "l0_s", "l1_q", "l1_s"])
+              + ["%s_%s" % (n, w) for n in ("l0", "l1", "e") for w in "qs"])
+
+GIVEN = {0: 3, 1: 0}
 
 
 def _count(mask):
@@ -43,48 +45,70 @@ def rank_program(g, core, T, topo):
         return
     R = T.cores
     S = T.sem
+    v, t, a, sy = g.vector, g.tensor, g.scalar, g.sync
     left = [0]
 
-    def codes(n):
-        return T["q" + n][:].bitcast(dt.uint8)
+    def view(what, n, lo=0, n_cols=NW):
+        p = T[what + n][:, lo:lo + n_cols]
+        return p.bitcast(dt.uint8) if what == "q" else p
 
-    def scales(n):
-        return T["s" + n][:]
+    def piece(n, i):
+        return T["q" + n][:, NW * i:NW * i + NW], T["s" + n][:, NW * i:NW * i + NW]
 
-    def send(dst, what, land, src, mask):
-        view = codes if what == "q" else scales
+    def send(dst, what, land, src, mask, lo=0, n_cols=NW):
         rid, pid, _ = topo.addr(dst)
-        g.remote_dma(out_ap=view(land), in_ap=view(src), remote_sem=S["%s_%s" % (land, what)], local_sem=S["left"],
+        g.remote_dma(out_ap=view(what, land, lo, n_cols), in_ap=view(what, src, lo, n_cols),
+                     remote_sem=S["%s_%s" % (land, what)], local_sem=S["left"],
                      pid=pid, routing_id=rid, dma_engine_mask=mask)
         left[0] += _count(mask)
 
     def send_two(pairs, what, land, src):
-        view = codes if what == "q" else scales
         tr = []
         for dst, mask in pairs:
             rid, pid, _ = topo.addr(dst)
-            tr.append(RemoteDMATransfer(src=view(src), dst=view(land), dst_ids=[DstId(rid=rid, pnc=pid)],
+            tr.append(RemoteDMATransfer(src=view(what, src), dst=view(what, land), dst_ids=[DstId(rid=rid, pnc=pid)],
                                         dma_engine_mask=mask, remote_sem=S["%s_%s" % (land, what)]))
             left[0] += _count(mask)
         g.remote_dma_fused(tr, local_sem=S["left"])
 
     m_far0 = topo.mask(R[0], R[2])
     m_near0 = topo.mask(R[0], R[1]) & ~m_far0
+    m_01 = topo.mask(R[0], R[1])
     m_10 = topo.mask(R[1], R[0])
     m_1h = topo.mask(R[1], helper)
     m_h2 = topo.mask(helper, R[2])
     m_03 = topo.mask(R[0], R[3])
     m_23 = topo.mask(R[2], R[3])
     arrive = {0: {"l1": m_10}, 1: {"l0": m_near0}, 2: {"l0": m_far0, "l1": m_h2}, 3: {"l0": m_23, "l1": m_03}}
+    arrive_e = {0: _count(m_10) + _count(m_h2), 1: _count(m_01) + _count(m_h2)}
+
+    def make_z():
+        v.memset(T.z[:], 1.0).then_inc(S.z_one, 1)
+        g.wait_ge(S.z_one, 1)
+        g.affine_select(T.z[:], T.z[:], [[-1, W + 4]], AluOpType.is_equal, 0.0, 3, 4).then_inc(S.z_sel, 1)
+        v.wait_ge(S.z_sel, 1)
+
+    def selector(i, sem):
+        qe, se = piece("e", i)
+        v.quantize_mx(qe, se, T.z[:, 3 - i:3 - i + W]).then_inc(sem, 1)
+
+    def give(i, dst, half, mask):
+        for what in ("q", "s"):
+            send(dst, what, "e", "e", mask, NW * i + half * (NW // 2), NW // 2)
 
     if rank is None:
+        make_z()
+        for r in (0, 1):
+            selector(GIVEN[r], S.q_e)
+        g.wait_ge(S.q_e, 2)
+        for r in (0, 1):
+            give(GIVEN[r], R[r], 1, m_h2)
         for what in ("q", "s"):
             g.wait_ge(S["l1_" + what], _count(m_1h))
             send(R[2], what, "l1", "l1", m_h2)
         g.wait_ge(S.left, left[0])
         return
 
-    v, t, a, sy = g.vector, g.tensor, g.scalar, g.sync
     COPY = ActivationFunctionType.Copy
 
     def bank(i):
@@ -92,9 +116,6 @@ def rank_program(g, core, T, topo):
 
     def col(buf, i):
         return T[buf][:, i:W:4]
-
-    def piece(n, i):
-        return T["q" + n][:, NW * i:NW * i + NW], T["s" + n][:, NW * i:NW * i + NW]
 
     def product(i, dest, stop):
         qa, sa = piece("a", i)
@@ -107,9 +128,14 @@ def rank_program(g, core, T, topo):
     a.dma_start(T.ta[:, 0:3 * W], T.a[:, 0:3 * W]).then_inc(S.ld_a, 16)
     sy.dma_start(T.ta[:, 3 * W:4 * W], T.a[:, 3 * W:4 * W]).then_inc(S.ld_a3, 16)
 
-    v.memset(T.z[:], 1.0).then_inc(S.z_one, 1)
-    g.wait_ge(S.z_one, 1)
-    g.affine_select(T.z[:], T.z[:], [[-1, W + 4]], AluOpType.is_equal, 0.0, 3, 4).then_inc(S.z_sel, 1)
+    make_z()
+    mine = [0, 1, 2, 3]
+    if rank in GIVEN:
+        other = 1 - rank
+        mine = [i for i in mine if i not in (GIVEN[rank], GIVEN[other])]
+        selector(GIVEN[other], S.q_e0)
+        g.wait_ge(S.q_e0, 1)
+        give(GIVEN[other], R[other], 0, m_01 if rank == 0 else m_10)
 
     v.wait_ge(S.ld_b, 16)
     v.quantize_mx(T.qb[:], T.sb[:], T.tb[:]).then_inc(S.q_b, 1)
@@ -152,10 +178,8 @@ def rank_program(g, core, T, topo):
             for what in ("q", "s"):
                 send(R[3], what, "l0", "h", m_23)
 
-    v.wait_ge(S.z_sel, 1)
-    for i in range(4):
-        qe, se = piece("e", i)
-        v.quantize_mx(qe, se, T.z[:, 3 - i:3 - i + W]).then_inc(S.q_e, 1)
+    for i in mine:
+        selector(i, S.q_e)
 
     if rank == 0:
         a.wait_ge(S.ch3, 1)
@@ -165,7 +189,11 @@ def rank_program(g, core, T, topo):
             sy.wait_ge(S["cy%d" % i], 1)
         sy.dma_start(T.y[:], T.yt[:]).then_inc(S.stored, 16)
 
-    t.wait_ge(S.q_e, 4)
+    t.wait_ge(S.q_e, len(mine))
+    if rank in GIVEN:
+        t.wait_ge(S.q_e0, 1)
+        for what in ("q", "s"):
+            t.wait_ge(S["e_" + what], arrive_e[rank])
     lands = sorted(arrive[rank])
     for land in lands:
         for what in ("q", "s"):

@@ -3,119 +3,131 @@ from concourse.mybir import dt, AluOpType, ActivationFunctionType
 
 W = 512
 NW = 128
+HW = NW // 2
 BANK = 512
 
 SCRATCH = {
     "ta": ("sbuf", [128, 4 * W], "bfloat16"),
     "tb": ("sbuf", [128, 2 * W], "bfloat16"),
+    "o": ("sbuf", [128, W + 4], "bfloat16"),
     "z": ("sbuf", [128, W + 4], "bfloat16"),
     "h": ("sbuf", [128, W], "bfloat16"),
-    "hs": ("sbuf", [128, W], "bfloat16"),
     "yt": ("sbuf", [128, W], "float32"),
     "ps": ("psum", [128, 8 * BANK], "float32"),
 }
-for _n, _w in (("a", 4 * NW), ("b", 2 * NW), ("e", 4 * NW), ("h", NW), ("s", NW), ("l0", NW), ("l1", NW)):
+for _n, _w in (("a", 4 * NW), ("b", 2 * NW), ("e", 4 * NW), ("h", NW), ("s", NW), ("p", NW), ("l1", NW),
+               ("l0", NW + HW)):
     SCRATCH["q" + _n] = ("sbuf", [128, _w], "float8_e4m3fn_x4")
     SCRATCH["s" + _n] = ("sbuf", [128, _w], "uint8")
 
-SEMAPHORES = (["ld_b", "ld_a", "ld_a3", "z_one", "z_sel", "q_b", "q_e", "q_e0", "q_h", "q_s", "stored", "left"]
-              + ["%s%d" % (n, i) for n in ("q_a", "mm", "ch", "cy", "cs", "fin") for i in range(4)]
-              + ["%s_%s" % (n, w) for n in ("l0", "l1", "e") for w in "qs"])
-
-GIVEN = {0: 3, 1: 0}
+SEMAPHORES = (["ld_b", "o_mem", "z_sel", "q_z", "q_b", "q_e", "q_h", "q_s", "stored", "left"]
+              + ["%s%d" % (n, i) for n in ("ld_a", "q_a", "mm", "ml", "ch", "cy", "cs", "fin") for i in range(4)]
+              + ["%s_%s" % (n, w) for n in ("zr", "e", "lo", "hi", "l0", "l1", "pl", "ph") for w in "qs"])
 
 
 def _count(mask):
     return bin(mask).count("1")
 
 
-def _helper(T, topo):
-    c1, c2 = T.cores[1], T.cores[2]
+def _halves(mask):
+    bits = [1 << k for k in range(mask.bit_length()) if mask >> k & 1]
+    return sum(bits[0::2]), sum(bits[1::2])
+
+
+def _helper(T, topo, dst):
     for c in range(128):
-        if (topo.chip(c) == topo.chip(c1) and topo.die(c) == topo.die(c1) and T.rank_of(c) is None
-                and topo.may_write(c, c2)):
+        if (topo.chip(c) == topo.chip(T.cores[1]) and topo.die(c) == topo.die(dst) and T.rank_of(c) is None
+                and topo.may_write(c, dst)):
             return c
     return None
 
 
 def rank_program(g, core, T, topo):
-    rank = T.rank_of(core)
-    helper = _helper(T, topo)
-    if rank is None and core != helper:
-        return
     R = T.cores
+    rank = T.rank_of(core)
+    help2, help3 = _helper(T, topo, R[2]), _helper(T, topo, R[3])
+    if rank is None and core not in (help2, help3):
+        return
     S = T.sem
     v, t, a, sy = g.vector, g.tensor, g.scalar, g.sync
     left = [0]
 
-    def view(what, n, lo=0, n_cols=NW):
+    def view(what, n, lo, n_cols):
         p = T[what + n][:, lo:lo + n_cols]
         return p.bitcast(dt.uint8) if what == "q" else p
+
+    def ship(dests, src, lo, n_cols, sem, after=None):
+        for what in ("q", "s"):
+            if after:
+                g.wait_ge(S["%s_%s" % (after[0], what)], after[1])
+            arr = S["%s_%s" % (sem, what)]
+            tr = []
+            for dst, land, at, mask in dests:
+                rid, pid, _ = topo.addr(dst)
+                left[0] += _count(mask)
+                if len(dests) == 1:
+                    g.remote_dma(out_ap=view(what, land, at, n_cols), in_ap=view(what, src, lo, n_cols),
+                                 remote_sem=arr, local_sem=S.left, pid=pid, routing_id=rid, dma_engine_mask=mask)
+                else:
+                    tr.append(RemoteDMATransfer(src=view(what, src, lo, n_cols), dst=view(what, land, at, n_cols),
+                                                dst_ids=[DstId(rid=rid, pnc=pid)], dma_engine_mask=mask,
+                                                remote_sem=arr))
+            if tr:
+                g.remote_dma_fused(tr, local_sem=S.left)
+
+    m_far = topo.mask(R[0], R[2]) & topo.mask(R[0], R[3])
+    m_far2, m_far3 = _halves(m_far)
+    m_near = topo.mask(R[0], R[1]) & ~m_far
+    m_1 = topo.mask(R[1], help2) & topo.mask(R[1], help3)
+    m_1h2, m_1h3 = _halves(m_1)
+    m_h2 = topo.mask(help2, R[2])
+    m_h3 = topo.mask(help3, R[3])
+    m_23 = topo.mask(R[2], R[3])
+
+    ZQ = HW // 2
+    GIVEN = 3
+
+    def zeros(codes, scales):
+        v.wait_ge(S.o_mem, 1)
+        v.quantize_mx(codes, scales, T.o[:, 0:W]).then_inc(S.q_z, 1)
+
+    def make_z():
+        g.wait_ge(S.o_mem, 1)
+        g.affine_select(T.z[:], T.o[:], [[-1, W + 4]], AluOpType.not_equal, 1.0, 3, 4).then_inc(S.z_sel, 1)
 
     def piece(n, i):
         return T["q" + n][:, NW * i:NW * i + NW], T["s" + n][:, NW * i:NW * i + NW]
 
-    def send(dst, what, land, src, mask, lo=0, n_cols=NW):
-        rid, pid, _ = topo.addr(dst)
-        g.remote_dma(out_ap=view(what, land, lo, n_cols), in_ap=view(what, src, lo, n_cols),
-                     remote_sem=S["%s_%s" % (land, what)], local_sem=S["left"],
-                     pid=pid, routing_id=rid, dma_engine_mask=mask)
-        left[0] += _count(mask)
-
-    def send_two(pairs, what, land, src):
-        tr = []
-        for dst, mask in pairs:
-            rid, pid, _ = topo.addr(dst)
-            tr.append(RemoteDMATransfer(src=view(what, src), dst=view(what, land), dst_ids=[DstId(rid=rid, pnc=pid)],
-                                        dma_engine_mask=mask, remote_sem=S["%s_%s" % (land, what)]))
-            left[0] += _count(mask)
-        g.remote_dma_fused(tr, local_sem=S["left"])
-
-    m_far0 = topo.mask(R[0], R[2])
-    m_near0 = topo.mask(R[0], R[1]) & ~m_far0
-    m_01 = topo.mask(R[0], R[1])
-    m_10 = topo.mask(R[1], R[0])
-    m_1h = topo.mask(R[1], helper)
-    m_h2 = topo.mask(helper, R[2])
-    m_03 = topo.mask(R[0], R[3])
-    m_23 = topo.mask(R[2], R[3])
-    arrive = {0: {"l1": m_10}, 1: {"l0": m_near0}, 2: {"l0": m_far0, "l1": m_h2}, 3: {"l0": m_23, "l1": m_03}}
-    arrive_e = {0: _count(m_10) + _count(m_h2), 1: _count(m_01) + _count(m_h2)}
-
-    def make_z():
-        v.memset(T.z[:], 1.0).then_inc(S.z_one, 1)
-        g.wait_ge(S.z_one, 1)
-        g.affine_select(T.z[:], T.z[:], [[-1, W + 4]], AluOpType.is_equal, 0.0, 3, 4).then_inc(S.z_sel, 1)
+    def selectors(which):
         v.wait_ge(S.z_sel, 1)
+        for i in which:
+            qe, se = piece("e", i)
+            v.quantize_mx(qe, se, T.z[:, 3 - i:3 - i + W]).then_inc(S.q_e, 1)
 
-    def selector(i, sem):
-        qe, se = piece("e", i)
-        v.quantize_mx(qe, se, T.z[:, 3 - i:3 - i + W]).then_inc(sem, 1)
+    if core == help2:
+        ship([(R[2], "l0", HW + ZQ, m_h2)], "l0", HW + ZQ, ZQ, "zr", after=("zr", _count(m_1)))
+        ship([(R[2], "l1", 0, m_h2)], "l1", 0, NW, "l1", after=("l1", _count(m_1h2)))
+        g.wait_ge(S.left, left[0])
+        return
 
-    def give(i, dst, half, mask):
-        for what in ("q", "s"):
-            send(dst, what, "e", "e", mask, NW * i + half * (NW // 2), NW // 2)
+    v.memset(T.o[:], 0.0).then_inc(S.o_mem, 1)
 
-    if rank is None:
+    if core == help3:
         make_z()
-        for r in (0, 1):
-            selector(GIVEN[r], S.q_e)
-        g.wait_ge(S.q_e, 2)
-        for r in (0, 1):
-            give(GIVEN[r], R[r], 1, m_h2)
-        for what in ("q", "s"):
-            g.wait_ge(S["l1_" + what], _count(m_1h))
-            send(R[2], what, "l1", "l1", m_h2)
+        selectors([GIVEN])
+        g.wait_ge(S.q_e, 1)
+        ship([(R[1], "e", NW * GIVEN, m_h3)], "e", NW * GIVEN, NW, "e")
+        ship([(R[3], "l1", 0, m_h3)], "l1", 0, NW, "l1", after=("l1", _count(m_1h3)))
         g.wait_ge(S.left, left[0])
         return
 
     COPY = ActivationFunctionType.Copy
 
-    def bank(i):
-        return T.ps[:, BANK * i:BANK * i + NW]
+    def bank(i, n=NW):
+        return T.ps[:, BANK * i:BANK * i + n]
 
-    def col(buf, i):
-        return T[buf][:, i:W:4]
+    def col(buf, i, end=W):
+        return T[buf][:, i:end:4]
 
     def product(i, dest, stop):
         qa, sa = piece("a", i)
@@ -124,27 +136,36 @@ def rank_program(g, core, T, topo):
             m = t.matmul_mx(bank(dest), qa, sa, qb, sb, k == 0, stop and k == 1)
         return m
 
-    sy.dma_start(T.tb[:], T.b[:]).then_inc(S.ld_b, 16)
-    a.dma_start(T.ta[:, 0:3 * W], T.a[:, 0:3 * W]).then_inc(S.ld_a, 16)
-    sy.dma_start(T.ta[:, 3 * W:4 * W], T.a[:, 3 * W:4 * W]).then_inc(S.ld_a3, 16)
+    def unpack(i, dest, land, at, start, stop):
+        qe, se = piece("e", i)
+        return t.matmul_mx(bank(dest), qe, se, T["q" + land][:, at:at + NW], T["s" + land][:, at:at + NW], start, stop)
 
-    make_z()
-    mine = [0, 1, 2, 3]
-    if rank in GIVEN:
-        other = 1 - rank
-        mine = [i for i in mine if i not in (GIVEN[rank], GIVEN[other])]
-        selector(GIVEN[other], S.q_e0)
-        g.wait_ge(S.q_e0, 1)
-        give(GIVEN[other], R[other], 0, m_01 if rank == 0 else m_10)
+    def landed(sem, n):
+        for what in ("q", "s"):
+            t.wait_ge(S["%s_%s" % (sem, what)], n)
+
+    sy.dma_start(T.tb[:], T.b[:]).then_inc(S.ld_b, 16)
+    for i in range(4):
+        (a if i % 2 == 0 else sy).dma_start(T.ta[:, W * i:W * i + W], T.a[:, W * i:W * i + W]).then_inc(S["ld_a%d" % i], 16)
+
+    if rank < 2:
+        zeros(T.qs[:], T.ss[:])
+        g.wait_ge(S.q_z, 1)
+        if rank == 0:
+            ship([(R[2], "l0", HW, m_far)], "s", 0, ZQ, "zr")
+        else:
+            ship([(help2, "l0", HW + ZQ, m_1)], "s", ZQ, ZQ, "zr")
+    else:
+        if rank == 3:
+            zeros(T.ql0[:, 0:NW], T.sl0[:, 0:NW])
+        make_z()
+        selectors(range(4))
 
     v.wait_ge(S.ld_b, 16)
     v.quantize_mx(T.qb[:], T.sb[:], T.tb[:]).then_inc(S.q_b, 1)
     t.wait_ge(S.q_b, 1)
     for i in range(4):
-        if i == 0:
-            v.wait_ge(S.ld_a, 16)
-        if i == 3:
-            v.wait_ge(S.ld_a3, 16)
+        v.wait_ge(S["ld_a%d" % i], 16)
         qa, sa = piece("a", i)
         v.quantize_mx(qa, sa, T.ta[:, W * i:W * i + W]).then_inc(S["q_a%d" % i], 1)
         t.wait_ge(S["q_a%d" % i], 1)
@@ -152,7 +173,7 @@ def rank_program(g, core, T, topo):
             product(i, i, True).then_inc(S["mm%d" % i], 1)
         else:
             product(i, 4 + i, False)
-    if rank < 3:
+    if rank in (1, 2):
         for i in range(4):
             product(i, 4 + i, False)
 
@@ -166,64 +187,73 @@ def rank_program(g, core, T, topo):
             v.wait_ge(S["ch%d" % i], 1)
         v.quantize_mx(T.qh[:], T.sh[:], T.h[:]).then_inc(S.q_h, 1)
         g.wait_ge(S.q_h, 1)
-        if rank == 0:
-            for what in ("q", "s"):
-                send_two([(R[2], m_far0), (R[1], m_near0)], what, "l0", "h")
-        if rank == 1:
-            for what in ("q", "s"):
-                send(R[0], what, "l1", "h", m_10)
-            for what in ("q", "s"):
-                send(helper, what, "l1", "h", m_1h)
-        if rank == 2:
-            for what in ("q", "s"):
-                send(R[3], what, "l0", "h", m_23)
-
-    for i in mine:
-        selector(i, S.q_e)
 
     if rank == 0:
+        ship([(R[2], "l0", 0, m_far)], "h", 0, HW, "lo")
+        ship([(R[2], "l0", NW, m_far2), (R[3], "l0", NW, m_far3)], "h", HW, HW, "hi")
+        ship([(R[1], "l0", 0, m_near)], "h", 0, NW, "l0")
         a.wait_ge(S.ch3, 1)
         for i in range(4):
             a.wait_ge(S["mm%d" % i], 1)
             a.activation(col("yt", i), bank(i), COPY).then_inc(S["cy%d" % i], 1)
-            sy.wait_ge(S["cy%d" % i], 1)
-        sy.dma_start(T.y[:], T.yt[:]).then_inc(S.stored, 16)
-
-    t.wait_ge(S.q_e, len(mine))
-    if rank in GIVEN:
-        t.wait_ge(S.q_e0, 1)
-        for what in ("q", "s"):
-            t.wait_ge(S["e_" + what], arrive_e[rank])
-    lands = sorted(arrive[rank])
-    for land in lands:
-        for what in ("q", "s"):
-            t.wait_ge(S["%s_%s" % (land, what)], _count(arrive[rank][land]))
-        ql, sl = T["q" + land][:], T["s" + land][:]
+    if rank == 1:
+        ship([(help3, "l1", 0, m_1h3), (help2, "l1", 0, m_1h2)], "h", 0, NW, "l1")
+        make_z()
+        selectors([i for i in range(4) if i != GIVEN])
+        t.wait_ge(S.q_e, 3)
+        landed("e", _count(m_h3))
+        landed("l0", _count(m_near))
         for i in range(4):
-            qe, se = piece("e", i)
-            last = land == lands[-1]
-            m = t.matmul_mx(bank(4 + i), qe, se, ql, sl, False, last)
-            if last:
-                m.then_inc(S["fin%d" % i], 1)
-
-    buf, cs = ("hs", "cs%d") if rank == 0 else ("yt", "cy%d")
-    for i in (0, 2):
-        a.wait_ge(S["fin%d" % i], 1)
-        a.activation(col(buf, i), bank(4 + i), COPY).then_inc(S[cs % i], 1)
-    for i in (1, 3):
-        v.wait_ge(S["fin%d" % i], 1)
-        v.tensor_copy(col(buf, i), bank(4 + i)).then_inc(S[cs % i], 1)
-    if rank == 0:
+            unpack(i, 4 + i, "l0", 0, False, True).then_inc(S["fin%d" % i], 1)
+    if rank == 2:
+        ship([(R[3], "p", HW, m_23)], "h", HW, HW, "ph")
+        t.wait_ge(S.q_e, 4)
+        landed("zr", _count(m_far) + _count(m_h2))
+        landed("lo", _count(m_far))
         for i in range(4):
-            v.wait_ge(S[cs % i], 1)
-        v.quantize_mx(T.qs[:], T.ss[:], T.hs[:]).then_inc(S.q_s, 1)
+            t.wait_ge(S["ch%d" % i], 1)
+            unpack(i, i, "l0", 0, True, True).then_inc(S["ml%d" % i], 1)
+        v.wait_ge(S.q_h, 1)
+        for i in range(4):
+            v.wait_ge(S["ml%d" % i], 1)
+            v.tensor_tensor(col("h", i, 4 * HW), bank(i, HW), col("h", i, 4 * HW), AluOpType.add).then_inc(S["cs%d" % i], 1)
+        for i in range(4):
+            v.wait_ge(S["cs%d" % i], 1)
+        v.quantize_mx(T.qs[:], T.ss[:], T.h[:]).then_inc(S.q_s, 1)
         g.wait_ge(S.q_s, 1)
-        for what in ("q", "s"):
-            send(R[3], what, "l1", "s", m_03)
-    else:
+        ship([(R[3], "p", 0, m_23)], "s", 0, HW, "pl")
         for i in range(4):
-            sy.wait_ge(S[cs % i], 1)
-        sy.dma_start(T.y[:], T.yt[:]).then_inc(S.stored, 16)
+            unpack(i, 4 + i, "l0", 0, False, False)
+        landed("hi", _count(m_far2))
+        for i in range(4):
+            unpack(i, 4 + i, "l0", HW, False, False)
+        landed("l1", _count(m_h2))
+        for i in range(4):
+            unpack(i, 4 + i, "l1", 0, False, True).then_inc(S["fin%d" % i], 1)
+    if rank == 3:
+        t.wait_ge(S.q_e, 4)
+        t.wait_ge(S.q_z, 1)
+        landed("hi", _count(m_far3))
+        for i in range(4):
+            unpack(i, 4 + i, "l0", HW, False, False)
+        landed("l1", _count(m_h3))
+        for i in range(4):
+            unpack(i, 4 + i, "l1", 0, False, False)
+        landed("ph", _count(m_23))
+        landed("pl", _count(m_23))
+        for i in range(4):
+            unpack(i, 4 + i, "p", 0, False, True).then_inc(S["fin%d" % i], 1)
+
+    if rank > 0:
+        for i in (0, 2):
+            a.wait_ge(S["fin%d" % i], 1)
+            a.activation(col("yt", i), bank(4 + i), COPY).then_inc(S["cy%d" % i], 1)
+        for i in (1, 3):
+            v.wait_ge(S["fin%d" % i], 1)
+            v.tensor_copy(col("yt", i), bank(4 + i)).then_inc(S["cy%d" % i], 1)
+    for i in range(4):
+        sy.wait_ge(S["cy%d" % i], 1)
+    sy.dma_start(T.y[:], T.yt[:]).then_inc(S.stored, 16)
     sy.wait_ge(S.stored, 16)
     if left[0]:
         g.wait_ge(S.left, left[0])

@@ -4,25 +4,31 @@ from concourse.mybir import dt, AluOpType, ActivationFunctionType
 W = 512
 NW = 128
 HW = NW // 2
+HE = W // 2
 BANK = 512
+PAD = HW // 2
+GIVEN = 3
 
 SCRATCH = {
     "ta": ("sbuf", [128, 4 * W], "bfloat16"),
     "tb": ("sbuf", [128, 2 * W], "bfloat16"),
     "o": ("sbuf", [128, W + 4], "bfloat16"),
     "z": ("sbuf", [128, W + 4], "bfloat16"),
-    "h": ("sbuf", [128, W], "bfloat16"),
+    "h": ("sbuf", [128, 3 * HE], "bfloat16"),
+    "h2": ("sbuf", [128, W], "bfloat16"),
     "yt": ("sbuf", [128, W], "float32"),
     "ps": ("psum", [128, 8 * BANK], "float32"),
 }
-for _n, _w in (("a", 4 * NW), ("b", 2 * NW), ("e", 4 * NW), ("h", NW), ("s", NW), ("p", NW), ("l1", NW),
-               ("l0", NW + HW)):
+for _n, _w in (("a", 4 * NW), ("b", 2 * NW), ("e", 4 * NW), ("h", NW), ("l", NW), ("z", NW), ("l0", 4 * HW),
+               ("l1", 6 * HW), ("p", 3 * HW)):
     SCRATCH["q" + _n] = ("sbuf", [128, _w], "float8_e4m3fn_x4")
     SCRATCH["s" + _n] = ("sbuf", [128, _w], "uint8")
 
-SEMAPHORES = (["ld_b", "o_mem", "z_sel", "q_z", "q_b", "q_e", "q_h", "q_s", "stored", "left"]
-              + ["%s%d" % (n, i) for n in ("ld_a", "q_a", "mm", "ml", "ch", "cy", "cs", "fin") for i in range(4)]
-              + ["%s_%s" % (n, w) for n in ("zr", "e", "lo", "hi", "l0", "l1", "pl", "ph") for w in "qs"])
+SEMAPHORES = (["ld_b", "o_mem", "h_mem", "h2_mem", "z_sel", "q_z", "q_b", "q_e", "q_l", "q_h", "q_s", "stored", "left"]
+              + ["%s%d" % (n, i) for n in ("ld_a", "q_a", "mm", "ml", "my", "ch", "cy", "cl", "cs", "fin")
+                 for i in range(4)]
+              + ["%s_%s" % (n, w) for n in ("e", "pad", "t0", "t0lo", "t0hi", "t1lo", "t1hi", "t2hi", "sum")
+                 for w in "qs"])
 
 
 def _count(mask):
@@ -34,10 +40,10 @@ def _halves(mask):
     return sum(bits[0::2]), sum(bits[1::2])
 
 
-def _helper(T, topo, dst):
+def _helper(T, topo, dst, taken=()):
     for c in range(128):
         if (topo.chip(c) == topo.chip(T.cores[1]) and topo.die(c) == topo.die(dst) and T.rank_of(c) is None
-                and topo.may_write(c, dst)):
+                and c not in taken and topo.may_write(c, dst)):
             return c
     return None
 
@@ -46,21 +52,23 @@ def rank_program(g, core, T, topo):
     R = T.cores
     rank = T.rank_of(core)
     help2, help3 = _helper(T, topo, R[2]), _helper(T, topo, R[3])
-    if rank is None and core not in (help2, help3):
+    helps = _helper(T, topo, R[3], (help2, help3))
+    if rank is None and core not in (help2, help3, helps):
         return
     S = T.sem
     v, t, a, sy = g.vector, g.tensor, g.scalar, g.sync
+    COPY = ActivationFunctionType.Copy
     left = [0]
 
     def view(what, n, lo, n_cols):
         p = T[what + n][:, lo:lo + n_cols]
         return p.bitcast(dt.uint8) if what == "q" else p
 
-    def ship(dests, src, lo, n_cols, sem, after=None):
-        for what in ("q", "s"):
-            if after:
-                g.wait_ge(S["%s_%s" % (after[0], what)], after[1])
+    def ship(dests, src, lo, n_cols, sem, kinds="qs", after=None):
+        for what in kinds:
             arr = S["%s_%s" % (sem, what)]
+            if after:
+                g.wait_ge(arr, after)
             tr = []
             for dst, land, at, mask in dests:
                 rid, pid, _ = topo.addr(dst)
@@ -76,184 +84,232 @@ def rank_program(g, core, T, topo):
                 g.remote_dma_fused(tr, local_sem=S.left)
 
     m_far = topo.mask(R[0], R[2]) & topo.mask(R[0], R[3])
-    m_far2, m_far3 = _halves(m_far)
     m_near = topo.mask(R[0], R[1]) & ~m_far
-    m_1 = topo.mask(R[1], help2) & topo.mask(R[1], help3)
+    m_1 = topo.mask(R[1], help2) & topo.mask(R[1], help3) & topo.mask(R[1], helps)
     m_1h2, m_1h3 = _halves(m_1)
     m_h2 = topo.mask(help2, R[2])
     m_h3 = topo.mask(help3, R[3])
+    m_hs = topo.mask(helps, R[2]) & topo.mask(helps, R[3])
+    m_hs2, m_hs3 = _halves(m_hs)
     m_23 = topo.mask(R[2], R[3])
+    m_21 = topo.mask(R[2], R[1])
 
-    ZQ = HW // 2
-    GIVEN = 3
+    given = {help3: (0, HW, m_h3), helps: (HW, PAD, m_hs), R[2]: (HW + PAD, PAD, m_21)}
 
-    def zeros(codes, scales):
-        v.wait_ge(S.o_mem, 1)
-        v.quantize_mx(codes, scales, T.o[:, 0:W]).then_inc(S.q_z, 1)
+    def cut(n, at):
+        return T["q" + n][:, at:at + NW], T["s" + n][:, at:at + NW]
+
+    def quantise(n, at, src, sem):
+        q, s = cut(n, at)
+        v.quantize_mx(q, s, src).then_inc(sem, 1)
 
     def make_z():
         g.wait_ge(S.o_mem, 1)
         g.affine_select(T.z[:], T.o[:], [[-1, W + 4]], AluOpType.not_equal, 1.0, 3, 4).then_inc(S.z_sel, 1)
 
-    def piece(n, i):
-        return T["q" + n][:, NW * i:NW * i + NW], T["s" + n][:, NW * i:NW * i + NW]
-
     def selectors(which):
         v.wait_ge(S.z_sel, 1)
-        for i in which:
-            qe, se = piece("e", i)
-            v.quantize_mx(qe, se, T.z[:, 3 - i:3 - i + W]).then_inc(S.q_e, 1)
+        for e in which:
+            quantise("e", NW * e, T.z[:, 3 - e:3 - e + W], S.q_e)
+
+    def give_selector(made):
+        lo, n, mask = given[core]
+        g.wait_ge(S.q_e, made)
+        ship([(R[1], "e", NW * GIVEN + lo, mask)], "e", NW * GIVEN + lo, n, "e")
+
+    def pass_on(kind, after, *dests):
+        ship([(dst, "l1", at, mask) for dst, at, mask in dests], "l1", HW, HW, "t1lo", kind, after)
+        ship([(dst, "l1", 0, mask) for dst, at, mask in dests], "l1", 0, HW, "t1hi", kind, after)
+        g.wait_ge(S.left, left[0])
+
+    AT2, AT3 = HW, NW + HW
 
     if core == help2:
-        ship([(R[2], "l0", HW + ZQ, m_h2)], "l0", HW + ZQ, ZQ, "zr", after=("zr", _count(m_1)))
-        ship([(R[2], "l1", 0, m_h2)], "l1", 0, NW, "l1", after=("l1", _count(m_1h2)))
-        g.wait_ge(S.left, left[0])
+        ship([(R[2], "l1", NW + PAD, m_h2)], "l1", NW, PAD, "pad", after=_count(m_1))
+        pass_on("q", _count(m_1h2), (R[2], AT2, m_h2))
         return
 
     v.memset(T.o[:], 0.0).then_inc(S.o_mem, 1)
 
-    if core == help3:
+    if rank is None:
         make_z()
         selectors([GIVEN])
-        g.wait_ge(S.q_e, 1)
-        ship([(R[1], "e", NW * GIVEN, m_h3)], "e", NW * GIVEN, NW, "e")
-        ship([(R[3], "l1", 0, m_h3)], "l1", 0, NW, "l1", after=("l1", _count(m_1h3)))
-        g.wait_ge(S.left, left[0])
+        give_selector(1)
+        if core == help3:
+            pass_on("q", _count(m_1h3), (R[3], AT3, m_h3))
+        else:
+            pass_on("s", _count(m_1), (R[2], AT2, m_hs2), (R[3], AT3, m_hs3))
         return
 
-    COPY = ActivationFunctionType.Copy
+    def bank(i, side=0, n=NW):
+        return T.ps[:, BANK * i + side:BANK * i + side + n]
 
-    def bank(i, n=NW):
-        return T.ps[:, BANK * i:BANK * i + n]
+    def tile(i):
+        at = HE if i < 2 else 0
+        return [(T.h[:, at + 2 * k + i % 2:at + HE:4], bank(i, HW * k, HW)) for k in range(2)]
 
-    def col(buf, i, end=W):
-        return T[buf][:, i:end:4]
+    def y_cols(e, hi):
+        at = HE * (e // 2)
+        return T.yt[:, at + e % 2 + 2 * hi:at + HE:4]
 
-    def product(i, dest, stop):
-        qa, sa = piece("a", i)
+    def product(i):
         for k in range(2):
-            qb, sb = piece("b", k)
-            m = t.matmul_mx(bank(dest), qa, sa, qb, sb, k == 0, stop and k == 1)
-        return m
+            m = t.matmul_mx(bank(i), *cut("a", NW * i), *cut("b", NW * k), k == 0, k == 1)
+        m.then_inc(S["mm%d" % i], 1)
 
-    def unpack(i, dest, land, at, start, stop):
-        qe, se = piece("e", i)
-        return t.matmul_mx(bank(dest), qe, se, T["q" + land][:, at:at + NW], T["s" + land][:, at:at + NW], start, stop)
+    def unpack(first_bank, land, at, start, stop, done=None, before=None):
+        for e in range(4):
+            if before:
+                t.wait_ge(S["%s%d" % (before, e)], 1)
+            m = t.matmul_mx(bank(first_bank + e), *cut("e", NW * e), *cut(land, at), start, stop)
+            if done:
+                m.then_inc(S["%s%d" % (done, e)], 1)
 
-    def landed(sem, n):
-        for what in ("q", "s"):
-            t.wait_ge(S["%s_%s" % (sem, what)], n)
+    def landed(sem, codes, scales=None):
+        t.wait_ge(S["%s_q" % sem], codes)
+        t.wait_ge(S["%s_s" % sem], scales or codes)
+
+    def copy(e, pieces, after):
+        q = v if e % 2 else a
+        q.wait_ge(S["%s%d" % (after, e)], 1)
+        for out, src, done in pieces:
+            m = v.tensor_copy(out, src) if e % 2 else a.activation(out, src, COPY)
+            m.then_inc(S["%s%d" % (done, e)], 1)
 
     sy.dma_start(T.tb[:], T.b[:]).then_inc(S.ld_b, 16)
     for i in range(4):
-        (a if i % 2 == 0 else sy).dma_start(T.ta[:, W * i:W * i + W], T.a[:, W * i:W * i + W]).then_inc(S["ld_a%d" % i], 16)
+        sy.dma_start(T.ta[:, W * i:W * i + W], T.a[:, W * i:W * i + W]).then_inc(S["ld_a%d" % i], 16)
 
     if rank < 2:
-        zeros(T.qs[:], T.ss[:])
+        v.wait_ge(S.o_mem, 1)
+        quantise("z", 0, T.o[:, 0:W], S.q_z)
         g.wait_ge(S.q_z, 1)
         if rank == 0:
-            ship([(R[2], "l0", HW, m_far)], "s", 0, ZQ, "zr")
+            ship([(R[2], "l1", NW, m_far)], "z", 0, PAD, "pad")
         else:
-            ship([(help2, "l0", HW + ZQ, m_1)], "s", ZQ, ZQ, "zr")
+            ship([(help2, "l1", NW, m_1)], "z", 0, PAD, "pad")
+            make_z()
     else:
-        if rank == 3:
-            zeros(T.ql0[:, 0:NW], T.sl0[:, 0:NW])
         make_z()
+        if rank == 2:
+            v.memset(T.h2[:, HE:W], 0.0).then_inc(S.h2_mem, 1)
+        else:
+            v.wait_ge(S.o_mem, 1)
+            quantise("p", HW, T.o[:, 0:W], S.q_z)
+    if rank < 3:
+        v.memset(T.h[:, 2 * HE:3 * HE], 0.0).then_inc(S.h_mem, 1)
+    if rank >= 2:
         selectors(range(4))
+    if rank == 2:
+        give_selector(4)
 
     v.wait_ge(S.ld_b, 16)
     v.quantize_mx(T.qb[:], T.sb[:], T.tb[:]).then_inc(S.q_b, 1)
     t.wait_ge(S.q_b, 1)
     for i in range(4):
+        if i == 3 and rank < 2:
+            v.wait_ge(S.h_mem, 1)
+            v.wait_ge(S.ch0, 2)
+            v.wait_ge(S.ch1, 2)
+            quantise("l", 0, T.h[:, HE:3 * HE], S.q_l)
         v.wait_ge(S["ld_a%d" % i], 16)
-        qa, sa = piece("a", i)
-        v.quantize_mx(qa, sa, T.ta[:, W * i:W * i + W]).then_inc(S["q_a%d" % i], 1)
+        quantise("a", NW * i, T.ta[:, W * i:W * i + W], S["q_a%d" % i])
         t.wait_ge(S["q_a%d" % i], 1)
-        if rank < 3:
-            product(i, i, True).then_inc(S["mm%d" % i], 1)
-        else:
-            product(i, 4 + i, False)
-    if rank in (1, 2):
-        for i in range(4):
-            product(i, 4 + i, False)
-
-    if rank < 3:
-        for i in range(3):
-            a.wait_ge(S["mm%d" % i], 1)
-            a.activation(col("h", i), bank(i), COPY).then_inc(S["ch%d" % i], 1)
-        v.wait_ge(S.mm3, 1)
-        v.tensor_copy(col("h", 3), bank(3)).then_inc(S.ch3, 1)
-        for i in range(4):
-            v.wait_ge(S["ch%d" % i], 1)
-        v.quantize_mx(T.qh[:], T.sh[:], T.h[:]).then_inc(S.q_h, 1)
-        g.wait_ge(S.q_h, 1)
+        product(i)
+        q = a if i < 3 else v
+        q.wait_ge(S["mm%d" % i], 1)
+        for out, src in tile(i):
+            m = a.activation(out, src, COPY) if i < 3 else v.tensor_copy(out, src)
+            m.then_inc(S["ch%d" % i], 1)
+    for i in range(4):
+        v.wait_ge(S["ch%d" % i], 2)
+    quantise(*(("l1", 2 * NW) if rank == 3 else ("h", 0)), T.h[:, 0:W], S.q_h)
 
     if rank == 0:
-        ship([(R[2], "l0", 0, m_far)], "h", 0, HW, "lo")
-        ship([(R[2], "l0", NW, m_far2), (R[3], "l0", NW, m_far3)], "h", HW, HW, "hi")
-        ship([(R[1], "l0", 0, m_near)], "h", 0, NW, "l0")
-        a.wait_ge(S.ch3, 1)
+        g.wait_ge(S.q_l, 1)
+        ship([(R[2], "l0", HW, m_far)], "l", 0, HW, "t0lo")
+        g.wait_ge(S.q_h, 1)
+        ship([(R[2], "l0", 0, m_far)], "h", 0, HW, "t0hi")
+        ship([(R[3], "l1", NW, m_far)], "h", 0, HW, "t0hi")
+        ship([(R[1], "l0", 0, m_near)], "h", 0, NW, "t0")
+        a.wait_ge(S.ch3, 2)
         for i in range(4):
             a.wait_ge(S["mm%d" % i], 1)
-            a.activation(col("yt", i), bank(i), COPY).then_inc(S["cy%d" % i], 1)
+            a.activation(T.yt[:, i:W:4], bank(i), COPY).then_inc(S["cy%d" % i], 1)
+        sy.wait_ge(S.left, left[0])
+
     if rank == 1:
-        ship([(help3, "l1", 0, m_1h3), (help2, "l1", 0, m_1h2)], "h", 0, NW, "l1")
-        make_z()
-        selectors([i for i in range(4) if i != GIVEN])
+        for at, src, done, sem in ((HW, "l", S.q_l, "t1lo"), (0, "h", S.q_h, "t1hi")):
+            g.wait_ge(done, 1)
+            ship([(help3, "l1", at, m_1h3), (help2, "l1", at, m_1h2)], src, 0, HW, sem, "q")
+            ship([(helps, "l1", at, m_1)], src, 0, HW, sem, "s")
+        selectors([e for e in range(4) if e != GIVEN])
         t.wait_ge(S.q_e, 3)
-        landed("e", _count(m_h3))
-        landed("l0", _count(m_near))
-        for i in range(4):
-            unpack(i, 4 + i, "l0", 0, False, True).then_inc(S["fin%d" % i], 1)
+        landed("e", sum(_count(m) for _, _, m in given.values()))
+        t.wait_ge(S.q_h, 1)
+        unpack(4, "h", 0, True, False)
+        landed("t0", _count(m_near))
+        unpack(4, "l0", 0, False, True, done="fin")
+
     if rank == 2:
-        ship([(R[3], "p", HW, m_23)], "h", HW, HW, "ph")
+        v.wait_ge(S.h_mem, 1)
+        quantise("l0", NW, T.h[:, HE:3 * HE], S.q_l)
+        g.wait_ge(S.q_h, 1)
+        ship([(R[3], "p", 0, m_23)], "h", 0, HW, "t2hi")
         t.wait_ge(S.q_e, 4)
-        landed("zr", _count(m_far) + _count(m_h2))
-        landed("lo", _count(m_far))
-        for i in range(4):
-            t.wait_ge(S["ch%d" % i], 1)
-            unpack(i, i, "l0", 0, True, True).then_inc(S["ml%d" % i], 1)
-        v.wait_ge(S.q_h, 1)
-        for i in range(4):
-            v.wait_ge(S["ml%d" % i], 1)
-            v.tensor_tensor(col("h", i, 4 * HW), bank(i, HW), col("h", i, 4 * HW), AluOpType.add).then_inc(S["cs%d" % i], 1)
-        for i in range(4):
-            v.wait_ge(S["cs%d" % i], 1)
-        v.quantize_mx(T.qs[:], T.ss[:], T.h[:]).then_inc(S.q_s, 1)
+        t.wait_ge(S.q_l, 1)
+        unpack(4, "l0", NW, True, False)
+        landed("t0lo", _count(m_far))
+        unpack(4, "l0", HW, False, True, done="ml")
+        v.wait_ge(S.h2_mem, 1)
+        for e in range(4):
+            copy(e, [(T.h2[:, e:HE:4], bank(4 + e, 0, HW), "cs")], "ml")
+        for e in range(4):
+            v.wait_ge(S["cs%d" % e], 1)
+        quantise("l", 0, T.h2[:], S.q_s)
         g.wait_ge(S.q_s, 1)
-        ship([(R[3], "p", 0, m_23)], "s", 0, HW, "pl")
-        for i in range(4):
-            unpack(i, 4 + i, "l0", 0, False, False)
-        landed("hi", _count(m_far2))
-        for i in range(4):
-            unpack(i, 4 + i, "l0", HW, False, False)
-        landed("l1", _count(m_h2))
-        for i in range(4):
-            unpack(i, 4 + i, "l1", 0, False, True).then_inc(S["fin%d" % i], 1)
+        ship([(R[3], "l1", HW, m_23)], "l", 0, HW, "sum")
+        t.wait_ge(S.q_h, 1)
+        unpack(0, "h", 0, True, False)
+        landed("t0hi", _count(m_far))
+        unpack(0, "l0", 0, False, False)
+        landed("t1lo", _count(m_h2), _count(m_hs2))
+        landed("pad", _count(m_far) + _count(m_h2))
+        unpack(4, "l1", HW, True, True, done="my", before="cs")
+        for e in range(4):
+            v.wait_ge(S["my%d" % e], 1)
+            v.tensor_tensor(y_cols(e, 0), bank(4 + e, 0, HW), T.h2[:, e:HE:4], AluOpType.add).then_inc(S["cl%d" % e], 1)
+        landed("t1hi", _count(m_h2), _count(m_hs2))
+        unpack(0, "l1", 0, False, True, done="fin")
+
     if rank == 3:
         t.wait_ge(S.q_e, 4)
+        t.wait_ge(S.q_h, 1)
+        unpack(0, "l1", 2 * NW, True, False)
         t.wait_ge(S.q_z, 1)
-        landed("hi", _count(m_far3))
-        for i in range(4):
-            unpack(i, 4 + i, "l0", HW, False, False)
-        landed("l1", _count(m_h3))
-        for i in range(4):
-            unpack(i, 4 + i, "l1", 0, False, False)
-        landed("ph", _count(m_23))
-        landed("pl", _count(m_23))
-        for i in range(4):
-            unpack(i, 4 + i, "p", 0, False, True).then_inc(S["fin%d" % i], 1)
+        landed("t2hi", _count(m_23))
+        unpack(0, "p", 0, False, False)
+        landed("t0hi", _count(m_far))
+        landed("t1lo", _count(m_h3), _count(m_hs3))
+        unpack(0, "l1", NW, False, False)
+        landed("sum", _count(m_23))
+        landed("t1hi", _count(m_h3), _count(m_hs3))
+        unpack(0, "l1", 0, False, True, done="fin")
 
     if rank > 0:
-        for i in (0, 2):
-            a.wait_ge(S["fin%d" % i], 1)
-            a.activation(col("yt", i), bank(4 + i), COPY).then_inc(S["cy%d" % i], 1)
-        for i in (1, 3):
-            v.wait_ge(S["fin%d" % i], 1)
-            v.tensor_copy(col("yt", i), bank(4 + i)).then_inc(S["cy%d" % i], 1)
+        b0 = 4 if rank == 1 else 0
+        for e in range(4):
+            lo = [] if rank == 2 else [(y_cols(e, 0), bank(b0 + e, HW, HW), "cl")]
+            copy(e, [(y_cols(e, 1), bank(b0 + e, 0, HW), "cy")] + lo, "fin")
     for i in range(4):
         sy.wait_ge(S["cy%d" % i], 1)
-    sy.dma_start(T.y[:], T.yt[:]).then_inc(S.stored, 16)
-    sy.wait_ge(S.stored, 16)
-    if left[0]:
+        if rank > 0:
+            sy.wait_ge(S["cl%d" % i], 1)
+            if i % 2:
+                at = HE * (i // 2)
+                sy.dma_start(T.y[:, at:at + HE], T.yt[:, at:at + HE]).then_inc(S.stored, 16)
+    if rank == 0:
+        sy.dma_start(T.y[:], T.yt[:]).then_inc(S.stored, 16)
+    sy.wait_ge(S.stored, 32 if rank > 0 else 16)
+    if rank in (1, 2):
         g.wait_ge(S.left, left[0])

from concourse.bass import DstId, RemoteDMATransfer
from concourse.mybir import dt, AluOpType, ActivationFunctionType

W = 512
NW = 128
HW = NW // 2
HE = W // 2
BANK = 512
PAD = HW // 2
GIVEN = 3

SCRATCH = {
    "ta": ("sbuf", [128, 4 * W], "bfloat16"),
    "tb": ("sbuf", [128, 2 * W], "bfloat16"),
    "o": ("sbuf", [128, W + 4], "bfloat16"),
    "z": ("sbuf", [128, W + 4], "bfloat16"),
    "h": ("sbuf", [128, 3 * HE], "bfloat16"),
    "h2": ("sbuf", [128, W], "bfloat16"),
    "yt": ("sbuf", [128, W], "float32"),
    "ps": ("psum", [128, 8 * BANK], "float32"),
}
for _n, _w in (("a", 4 * NW), ("b", 2 * NW), ("e", 4 * NW), ("h", NW), ("l", NW), ("z", NW), ("l0", 4 * HW),
               ("l1", 6 * HW), ("p", 3 * HW)):
    SCRATCH["q" + _n] = ("sbuf", [128, _w], "float8_e4m3fn_x4")
    SCRATCH["s" + _n] = ("sbuf", [128, _w], "uint8")

SEMAPHORES = (["ld_b", "o_mem", "h_mem", "h2_mem", "z_sel", "q_z", "q_b", "q_e", "q_l", "q_h", "q_s", "stored", "left"]
              + ["%s%d" % (n, i) for n in ("ld_a", "q_a", "mm", "ml", "my", "ch", "cy", "cl", "cs", "fin")
                 for i in range(4)]
              + ["%s_%s" % (n, w) for n in ("e", "pad", "t0", "t0lo", "t0hi", "t1lo", "t1hi", "t2hi", "sum")
                 for w in "qs"])


def _count(mask):
    return bin(mask).count("1")


def _halves(mask):
    bits = [1 << k for k in range(mask.bit_length()) if mask >> k & 1]
    return sum(bits[0::2]), sum(bits[1::2])


def _helper(T, topo, dst, taken=()):
    for c in range(128):
        if (topo.chip(c) == topo.chip(T.cores[1]) and topo.die(c) == topo.die(dst) and T.rank_of(c) is None
                and c not in taken and topo.may_write(c, dst)):
            return c
    return None


def rank_program(g, core, T, topo):
    R = T.cores
    rank = T.rank_of(core)
    help2, help3 = _helper(T, topo, R[2]), _helper(T, topo, R[3])
    helps = _helper(T, topo, R[3], (help2, help3))
    if rank is None and core not in (help2, help3, helps):
        return
    S = T.sem
    v, t, a, sy = g.vector, g.tensor, g.scalar, g.sync
    COPY = ActivationFunctionType.Copy
    left = [0]

    def view(what, n, lo, n_cols):
        p = T[what + n][:, lo:lo + n_cols]
        return p.bitcast(dt.uint8) if what == "q" else p

    def ship(dests, src, lo, n_cols, sem, kinds="qs", after=None):
        for what in kinds:
            arr = S["%s_%s" % (sem, what)]
            if after:
                g.wait_ge(arr, after)
            tr = []
            for dst, land, at, mask in dests:
                rid, pid, _ = topo.addr(dst)
                left[0] += _count(mask)
                if len(dests) == 1:
                    g.remote_dma(out_ap=view(what, land, at, n_cols), in_ap=view(what, src, lo, n_cols),
                                 remote_sem=arr, local_sem=S.left, pid=pid, routing_id=rid, dma_engine_mask=mask)
                else:
                    tr.append(RemoteDMATransfer(src=view(what, src, lo, n_cols), dst=view(what, land, at, n_cols),
                                                dst_ids=[DstId(rid=rid, pnc=pid)], dma_engine_mask=mask,
                                                remote_sem=arr))
            if tr:
                g.remote_dma_fused(tr, local_sem=S.left)

    m_far = topo.mask(R[0], R[2]) & topo.mask(R[0], R[3])
    m_near = topo.mask(R[0], R[1]) & ~m_far
    m_1 = topo.mask(R[1], help2) & topo.mask(R[1], help3) & topo.mask(R[1], helps)
    m_1h2, m_1h3 = _halves(m_1)
    m_h2 = topo.mask(help2, R[2])
    m_h3 = topo.mask(help3, R[3])
    m_hs = topo.mask(helps, R[2]) & topo.mask(helps, R[3])
    m_hs2, m_hs3 = _halves(m_hs)
    m_23 = topo.mask(R[2], R[3])
    m_21 = topo.mask(R[2], R[1])

    given = {help3: (0, HW, m_h3), helps: (HW, PAD, m_hs), R[2]: (HW + PAD, PAD, m_21)}

    def cut(n, at):
        return T["q" + n][:, at:at + NW], T["s" + n][:, at:at + NW]

    def quantise(n, at, src, sem):
        q, s = cut(n, at)
        v.quantize_mx(q, s, src).then_inc(sem, 1)

    def make_z():
        g.wait_ge(S.o_mem, 1)
        g.affine_select(T.z[:], T.o[:], [[-1, W + 4]], AluOpType.not_equal, 1.0, 3, 4).then_inc(S.z_sel, 1)

    def selectors(which):
        v.wait_ge(S.z_sel, 1)
        for e in which:
            quantise("e", NW * e, T.z[:, 3 - e:3 - e + W], S.q_e)

    def give_selector(made):
        lo, n, mask = given[core]
        g.wait_ge(S.q_e, made)
        ship([(R[1], "e", NW * GIVEN + lo, mask)], "e", NW * GIVEN + lo, n, "e")

    def pass_on(kind, after, *dests):
        ship([(dst, "l1", at, mask) for dst, at, mask in dests], "l1", HW, HW, "t1lo", kind, after)
        ship([(dst, "l1", 0, mask) for dst, at, mask in dests], "l1", 0, HW, "t1hi", kind, after)
        g.wait_ge(S.left, left[0])

    AT2, AT3 = HW, NW + HW

    if core == help2:
        ship([(R[2], "l1", NW + PAD, m_h2)], "l1", NW, PAD, "pad", after=_count(m_1))
        pass_on("q", _count(m_1h2), (R[2], AT2, m_h2))
        return

    v.memset(T.o[:], 0.0).then_inc(S.o_mem, 1)

    if rank is None:
        make_z()
        selectors([GIVEN])
        give_selector(1)
        if core == help3:
            pass_on("q", _count(m_1h3), (R[3], AT3, m_h3))
        else:
            pass_on("s", _count(m_1), (R[2], AT2, m_hs2), (R[3], AT3, m_hs3))
        return

    def bank(i, side=0, n=NW):
        return T.ps[:, BANK * i + side:BANK * i + side + n]

    def tile(i):
        at = HE if i < 2 else 0
        return [(T.h[:, at + 2 * k + i % 2:at + HE:4], bank(i, HW * k, HW)) for k in range(2)]

    def y_cols(e, hi):
        at = HE * (e // 2)
        return T.yt[:, at + e % 2 + 2 * hi:at + HE:4]

    def product(i):
        for k in range(2):
            m = t.matmul_mx(bank(i), *cut("a", NW * i), *cut("b", NW * k), k == 0, k == 1)
        m.then_inc(S["mm%d" % i], 1)

    def unpack(first_bank, land, at, start, stop, done=None, before=None):
        for e in range(4):
            if before:
                t.wait_ge(S["%s%d" % (before, e)], 1)
            m = t.matmul_mx(bank(first_bank + e), *cut("e", NW * e), *cut(land, at), start, stop)
            if done:
                m.then_inc(S["%s%d" % (done, e)], 1)

    def landed(sem, codes, scales=None):
        t.wait_ge(S["%s_q" % sem], codes)
        t.wait_ge(S["%s_s" % sem], scales or codes)

    def copy(e, pieces, after):
        q = v if e % 2 else a
        q.wait_ge(S["%s%d" % (after, e)], 1)
        for out, src, done in pieces:
            m = v.tensor_copy(out, src) if e % 2 else a.activation(out, src, COPY)
            m.then_inc(S["%s%d" % (done, e)], 1)

    sy.dma_start(T.tb[:], T.b[:]).then_inc(S.ld_b, 16)
    for i in range(4):
        sy.dma_start(T.ta[:, W * i:W * i + W], T.a[:, W * i:W * i + W]).then_inc(S["ld_a%d" % i], 16)

    if rank < 2:
        v.wait_ge(S.o_mem, 1)
        quantise("z", 0, T.o[:, 0:W], S.q_z)
        g.wait_ge(S.q_z, 1)
        if rank == 0:
            ship([(R[2], "l1", NW, m_far)], "z", 0, PAD, "pad")
        else:
            ship([(help2, "l1", NW, m_1)], "z", 0, PAD, "pad")
            make_z()
    else:
        make_z()
        if rank == 2:
            v.memset(T.h2[:, HE:W], 0.0).then_inc(S.h2_mem, 1)
        else:
            v.wait_ge(S.o_mem, 1)
            quantise("p", HW, T.o[:, 0:W], S.q_z)
    if rank < 3:
        v.memset(T.h[:, 2 * HE:3 * HE], 0.0).then_inc(S.h_mem, 1)
    if rank >= 2:
        selectors(range(4))
    if rank == 2:
        give_selector(4)

    v.wait_ge(S.ld_b, 16)
    v.quantize_mx(T.qb[:], T.sb[:], T.tb[:]).then_inc(S.q_b, 1)
    t.wait_ge(S.q_b, 1)
    for i in range(4):
        if i == 3 and rank < 2:
            v.wait_ge(S.h_mem, 1)
            v.wait_ge(S.ch0, 2)
            v.wait_ge(S.ch1, 2)
            quantise("l", 0, T.h[:, HE:3 * HE], S.q_l)
        v.wait_ge(S["ld_a%d" % i], 16)
        quantise("a", NW * i, T.ta[:, W * i:W * i + W], S["q_a%d" % i])
        t.wait_ge(S["q_a%d" % i], 1)
        product(i)
        q = a if i < 3 else v
        q.wait_ge(S["mm%d" % i], 1)
        for out, src in tile(i):
            m = a.activation(out, src, COPY) if i < 3 else v.tensor_copy(out, src)
            m.then_inc(S["ch%d" % i], 1)
    for i in range(4):
        v.wait_ge(S["ch%d" % i], 2)
    quantise(*(("l1", 2 * NW) if rank == 3 else ("h", 0)), T.h[:, 0:W], S.q_h)

    if rank == 0:
        g.wait_ge(S.q_l, 1)
        ship([(R[2], "l0", HW, m_far)], "l", 0, HW, "t0lo")
        g.wait_ge(S.q_h, 1)
        ship([(R[2], "l0", 0, m_far)], "h", 0, HW, "t0hi")
        ship([(R[3], "l1", NW, m_far)], "h", 0, HW, "t0hi")
        ship([(R[1], "l0", 0, m_near)], "h", 0, NW, "t0")
        a.wait_ge(S.ch3, 2)
        for i in range(4):
            a.wait_ge(S["mm%d" % i], 1)
            a.activation(T.yt[:, i:W:4], bank(i), COPY).then_inc(S["cy%d" % i], 1)
        sy.wait_ge(S.left, left[0])

    if rank == 1:
        for at, src, done, sem in ((HW, "l", S.q_l, "t1lo"), (0, "h", S.q_h, "t1hi")):
            g.wait_ge(done, 1)
            ship([(help3, "l1", at, m_1h3), (help2, "l1", at, m_1h2)], src, 0, HW, sem, "q")
            ship([(helps, "l1", at, m_1)], src, 0, HW, sem, "s")
        selectors([e for e in range(4) if e != GIVEN])
        t.wait_ge(S.q_e, 3)
        landed("e", sum(_count(m) for _, _, m in given.values()))
        t.wait_ge(S.q_h, 1)
        unpack(4, "h", 0, True, False)
        landed("t0", _count(m_near))
        unpack(4, "l0", 0, False, True, done="fin")

    if rank == 2:
        v.wait_ge(S.h_mem, 1)
        quantise("l0", NW, T.h[:, HE:3 * HE], S.q_l)
        g.wait_ge(S.q_h, 1)
        ship([(R[3], "p", 0, m_23)], "h", 0, HW, "t2hi")
        t.wait_ge(S.q_e, 4)
        t.wait_ge(S.q_l, 1)
        unpack(4, "l0", NW, True, False)
        landed("t0lo", _count(m_far))
        unpack(4, "l0", HW, False, True, done="ml")
        v.wait_ge(S.h2_mem, 1)
        for e in range(4):
            copy(e, [(T.h2[:, e:HE:4], bank(4 + e, 0, HW), "cs")], "ml")
        for e in range(4):
            v.wait_ge(S["cs%d" % e], 1)
        quantise("l", 0, T.h2[:], S.q_s)
        g.wait_ge(S.q_s, 1)
        ship([(R[3], "l1", HW, m_23)], "l", 0, HW, "sum")
        t.wait_ge(S.q_h, 1)
        unpack(0, "h", 0, True, False)
        landed("t0hi", _count(m_far))
        unpack(0, "l0", 0, False, False)
        landed("t1lo", _count(m_h2), _count(m_hs2))
        landed("pad", _count(m_far) + _count(m_h2))
        unpack(4, "l1", HW, True, True, done="my", before="cs")
        for e in range(4):
            v.wait_ge(S["my%d" % e], 1)
            v.tensor_tensor(y_cols(e, 0), bank(4 + e, 0, HW), T.h2[:, e:HE:4], AluOpType.add).then_inc(S["cl%d" % e], 1)
        landed("t1hi", _count(m_h2), _count(m_hs2))
        unpack(0, "l1", 0, False, True, done="fin")

    if rank == 3:
        t.wait_ge(S.q_e, 4)
        t.wait_ge(S.q_h, 1)
        unpack(0, "l1", 2 * NW, True, False)
        t.wait_ge(S.q_z, 1)
        landed("t2hi", _count(m_23))
        unpack(0, "p", 0, False, False)
        landed("t0hi", _count(m_far))
        landed("t1lo", _count(m_h3), _count(m_hs3))
        unpack(0, "l1", NW, False, False)
        landed("sum", _count(m_23))
        landed("t1hi", _count(m_h3), _count(m_hs3))
        unpack(0, "l1", 0, False, True, done="fin")

    if rank > 0:
        b0 = 4 if rank == 1 else 0
        for e in range(4):
            lo = [] if rank == 2 else [(y_cols(e, 0), bank(b0 + e, HW, HW), "cl")]
            copy(e, [(y_cols(e, 1), bank(b0 + e, 0, HW), "cy")] + lo, "fin")
    for i in range(4):
        sy.wait_ge(S["cy%d" % i], 1)
        if rank > 0:
            sy.wait_ge(S["cl%d" % i], 1)
            if i % 2:
                at = HE * (i // 2)
                sy.dma_start(T.y[:, at:at + HE], T.yt[:, at:at + HE]).then_inc(S.stored, 16)
    if rank == 0:
        sy.dma_start(T.y[:], T.yt[:]).then_inc(S.stored, 16)
    sy.wait_ge(S.stored, 32 if rank > 0 else 16)
    if rank in (1, 2):
        g.wait_ge(S.left, left[0])
